import numpy as np
import ml_dtypes


def mxq(x, axis, fmt="e4m3"):
    dtype, down = {"e4m3": (ml_dtypes.float8_e4m3fn, 7), "e5m2": (ml_dtypes.float8_e5m2, 14)}[fmt]
    v = np.moveaxis(np.asarray(x, np.float32).astype(ml_dtypes.bfloat16).astype(np.float64), axis, -1)
    blocks = v.reshape(v.shape[:-1] + (-1, 32))
    amax = np.abs(blocks).max(-1, keepdims=True)
    byte = np.maximum(np.where(amax > 0, np.frexp(amax)[1] - 1 + 127, 0) - down, 1)
    scale = np.exp2(byte - 127.0)
    codes = (blocks / scale).astype(np.float32).astype(dtype).astype(np.float64)
    return np.moveaxis((codes * scale).reshape(v.shape), -1, axis)


WIDE = False


def mx_kscale(k):
    if not WIDE:
        return np.ones(k)
    levels = np.array([10, -10, 5, -5, 0])
    if k % 512:
        return np.exp2(np.random.permutation(np.resize(levels, k // 32))).repeat(32)
    a = np.empty((k // 512, 16))
    for p in range(k // 512):
        a[p, :8] = np.random.permutation(np.resize(levels, 8))
        for g in range(8):
            far = levels[np.abs(levels - a[p, g]) >= 10]
            a[p, g + 8] = far[np.random.randint(len(far))]
    return np.exp2(a.ravel()).repeat(32)


def f64(x):
    return np.asarray(x).astype(np.float64)


def striped(idx):
    return np.tile(idx.reshape(-1, 16).T, (8, 1)).astype(np.uint16)


def unstriped(offs):
    return offs[:16].T.reshape(-1).astype(np.int64)


E2M1 = np.array([0.0, 0.5, 1.0, 1.5, 2.0, 3.0, 4.0, 6.0, -0.0, -0.5, -1.0, -1.5, -2.0, -3.0, -4.0, -6.0])


def pack_weight(w, fmt):
    k, n = w.shape
    w = f64(np.asarray(w, np.float32).astype(ml_dtypes.bfloat16)).reshape(k // 32, 32, n)
    amax = np.abs(w).max(1)
    if fmt == "e4m3":
        byte = np.frexp(amax)[1] - 1 + 127 - 7
    else:
        mant, ex = np.frexp(amax / 6.0)
        byte = np.where(mant > 0.5, ex, ex - 1) + 127
    byte = np.clip(np.where(amax > 0, byte, 1), 1, 254)
    scaled = (w * np.exp2(127.0 - byte)[:, None, :]).reshape(k, n).astype(np.float32)
    by_word = np.ascontiguousarray(scaled.reshape(k // 512, 128, 4, n).transpose(0, 1, 3, 2))
    if fmt == "e4m3":
        words = by_word.astype(ml_dtypes.float8_e4m3fn).view(np.uint8)
    else:
        c = by_word.astype(ml_dtypes.float4_e2m1fn).view(np.uint8) & 0xF
        words = (c[..., 0::2] | (c[..., 1::2] << 4)).reshape(k // 512, 128, 2 * n)
    return np.ascontiguousarray(words), np.ascontiguousarray(byte.astype(np.uint8).reshape(k // 512, 16, n))


def unpack_weight(words, scales, fmt):
    g, _, n = scales.shape
    words = np.ascontiguousarray(words).reshape(g, 128, n, -1)
    if fmt == "e4m3":
        vals = words.view(ml_dtypes.float8_e4m3fn).astype(np.float64)
    else:
        nib = np.empty((g, 128, n, 4), np.uint8)
        nib[..., 0::2] = words & 0xF
        nib[..., 1::2] = words >> 4
        vals = E2M1[nib]
    vals = vals * np.repeat(np.exp2(scales.astype(np.float64) - 127.0), 8, axis=1)[..., None]
    return vals.transpose(0, 1, 3, 2).reshape(g * 512, n)


def pack_table(v):
    words, scales = pack_weight(v, "e4m3")
    return np.concatenate([words.reshape(words.shape[0], -1), scales.reshape(scales.shape[0], -1)], axis=1)


def unpack_table(tab):
    g, t = tab.shape[0], tab.shape[1] // 528
    return unpack_weight(tab[:, :512 * t].reshape(g, 128, t, 4), tab[:, 512 * t:].reshape(g, 16, t), "e4m3")


def gelu(v):
    return 0.5 * v * (1.0 + np.tanh(np.sqrt(2.0 / np.pi) * (v + 0.044715 * v**3)))


K, M, T, S = 1024, 512, 4096, 2048


def setup_inputs():
    n = np.random.standard_normal
    s = mx_kscale(K)[:, None]
    w = n((K, M)) / np.sqrt(K) / s
    p_w4 = pack_weight(w[512:], "e2m1")
    return {
        "tab": pack_table(n((K, T)) * s),
        "w8": (w[:512]).astype(np.float32),
        "w4_words": p_w4[0],
        "w4_scales": p_w4[1],
        "b": (0.3 * n(512)).astype(np.float32),
        "wgo": np.tile(np.random.uniform(0.5, 2.0, S), (128, 1)).astype(np.float32),
        "offs": striped(np.random.permutation(T)[:S]),
        "offs2": striped(np.random.permutation(T)[:S]),
    }


def reference(tab, w8, w4_words, w4_scales, b, wgo, offs, offs2):
    tab_ = unpack_table(tab)[:, unstriped(offs)]
    w8_ = mxq(f64(w8), 0, "e4m3")
    w4_ = unpack_weight(w4_words, w4_scales, "e2m1")
    y = w8_.T @ tab_[:512] + w4_.T @ tab_[512:]
    out = np.zeros((M, T))
    out[:, unstriped(offs2)] = f64(wgo)[0] * (gelu(y + f64(b)[:, None]))
    return out

@@ -1,0 +1,169 @@
+from contextlib import ExitStack
+
+import concourse.mybir as mybir
+
+K, M, T, S = 1024, 512, 4096, 2048
+FLOPS = 2 * K * M * S
+
+F32 = mybir.dt.float32
+BF16 = mybir.dt.bfloat16
+I32 = mybir.dt.int32
+U32 = mybir.dt.uint32
+U16 = mybir.dt.uint16
+U8 = mybir.dt.uint8
+FP8X4 = mybir.dt.float8_e4m3fn_x4
+FP4X4 = mybir.dt.float4_e2m1fn_x4
+GELU = mybir.ActivationFunctionType.Gelu_apprx_tanh
+MULT = mybir.AluOpType.mult
+
+P = 128
+PACK = 4
+BANK = 512
+STRIPE = 16
+ROW_TILES = M // P
+HALF = M // 2
+FIRST = 512
+FP8_PLANE = 4
+SCALE_ROW = 512
+PASS_ROWS = 528
+GROUP_STEP = (PASS_ROWS + 4) // 7
+
+
+def tile_list_tabscat_o_gelu_kernel(
+    tc, tab, w8, w4_words, w4_scales, b, wgo, offs, offs2, out
+):
+    nc = tc.nc
+    with ExitStack() as ctx:
+        keep = ctx.enter_context(tc.tile_pool(name="keep", bufs=1))
+        psum = ctx.enter_context(tc.psum_pool(name="psum", bufs=8))
+
+        tab32 = tab.bitcast(I32)
+
+        def table_words(a):
+            return tab32[a, 0 : P * T].rearrange("(p t) -> p t", p=P)
+
+        tab_rows = tab32.rearrange("a (x w) -> (a x) w", w=T // 4)
+
+        def scale_groups(quadrant, groups):
+            first = SCALE_ROW + 4 * quadrant + 4 - GROUP_STEP
+            rows = tab_rows[first : first + GROUP_STEP * groups, :].rearrange("(u x) w -> u x w", u=groups)
+            return rows[:, GROUP_STEP - 4 :, :]
+
+        gather_list = keep.tile([P, S // STRIPE], U16, name="gather_list")
+        scatter_list = keep.tile([P, S // STRIPE], U16, name="scatter_list")
+        words = [keep.tile([P, T], I32, name=f"words{a}", align_bytes=64) for a in range(2)]
+        scale_window = keep.tile([P, T // 4], I32, name="scale_window", align_bytes=64)
+        windows = [keep.tile([P, T], F32, name=f"window{i}", align_bytes=64) for i in range(2)]
+        w8_raw = [keep.tile([P, PACK, HALF], F32, name=f"w8_raw{h}") for h in range(2)]
+        w8_bf16 = [keep.tile([P, HALF, PACK], BF16, name=f"w8_bf16_{h}", align_bytes=64) for h in range(2)]
+        w8_codes = [keep.tile([P, HALF], U32, name=f"w8_codes{h}", align_bytes=64) for h in range(2)]
+        w8_plane = [keep.tile([P, HALF], U8, name=f"w8_plane{h}", align_bytes=64) for h in range(2)]
+        w4_codes = keep.tile([P, 2 * M], U8, name="w4_codes", align_bytes=64)
+        w4_plane = keep.tile([P, M], U8, name="w4_plane", align_bytes=64)
+        bias = keep.tile([P, ROW_TILES], F32, name="bias")
+        weight = keep.tile([P, S], F32, name="weight")
+        warm_in = keep.tile([P, 8], F32, name="warm_in")
+        warm_out = keep.tile([P, 8], F32, name="warm_out")
+        picked0 = keep.tile([P, S], U32, name="picked0", align_bytes=64)
+        picked1_first = keep.tile([P, FIRST], U32, name="picked1_first", align_bytes=64)
+        picked1_rest = keep.tile([P, S - FIRST], U32, name="picked1_rest", align_bytes=64)
+        picked_scales = keep.tile([P, S], U8, name="picked_scales", align_bytes=64)
+
+        nc.gpsimd.memset(warm_in[:], 0.0)
+        nc.gpsimd.memset(w4_plane[:].bitcast(I32), 0)
+        nc.scalar.dma_start(scale_window[100:P, :], scale_groups(3, 7))
+        nc.scalar.activation(warm_out[:], warm_in[:], GELU)
+        for window in windows:
+            nc.vector.memset(window[:], 0.0)
+
+        w8_rows = w8.rearrange("(p j) n -> p j n", j=PACK)
+        nc.sync.dma_start(gather_list[:], offs)
+        nc.sync.dma_start(scale_window[0:4, :], tab_rows[PASS_ROWS + SCALE_ROW : PASS_ROWS + SCALE_ROW + 4, :])
+        for quadrant in range(3):
+            first = 32 * quadrant + FP8_PLANE
+            nc.sync.dma_start(scale_window[first : first + 32, :], scale_groups(quadrant, 8))
+        nc.sync.dma_start(words[0][:], table_words(0))
+        nc.sync.dma_start(w8_raw[0][:], w8_rows[:, :, 0:HALF])
+        nc.sync.dma_start(words[1][:], table_words(1))
+        nc.sync.dma_start(w4_codes[:].bitcast(I32), w4_words.bitcast(I32)[0])
+        with nc.allow_non_contiguous_dma(reason="one bias value a partition and row tile"):
+            nc.sync.dma_start(bias[:], b.rearrange("(m p) -> p m", p=P))
+        nc.sync.dma_start(scatter_list[:], offs2)
+        nc.sync.dma_start(weight[:], wgo)
+        nc.sync.dma_start(w8_raw[1][:], w8_rows[:, :, HALF:M])
+        w4_scale_rows = w4_scales.bitcast(I32)[0].rearrange("(q r) w -> r q w", r=4)
+        for r in range(4):
+            nc.gpsimd.dma_start(w4_plane[:].bitcast(I32)[r:P:32, :], w4_scale_rows[r])
+
+        def quantise_w8(h):
+            nc.scalar.copy(
+                w8_bf16[h][:].rearrange("p (c i) j -> p c j i", i=4),
+                w8_raw[h][:].rearrange("p j (c i) -> p c j i", i=4),
+            )
+            nc.vector.quantize_mx(
+                out=w8_codes[h][:].bitcast(FP8X4),
+                scales=w8_plane[h][:],
+                in_=w8_bf16[h][:].rearrange("p n j -> p (n j)"),
+            )
+
+        def list_slice(offsets, j0, j1):
+            return offsets[:, j0 // STRIPE : j1 // STRIPE]
+
+        nc.vector.tensor_copy(picked_scales[:], scale_window[:].bitcast(U8).indirect(gather_list[:]))
+        nc.vector.tensor_copy(picked0[:], words[0][:].bitcast(U32).indirect(gather_list[:]))
+        quantise_w8(0)
+        nc.vector.tensor_copy(
+            picked1_first[:], words[1][:].bitcast(U32).indirect(list_slice(gather_list, 0, FIRST))
+        )
+        nc.vector.tensor_copy(
+            picked1_rest[:], words[1][:].bitcast(U32).indirect(list_slice(gather_list, FIRST, S))
+        )
+
+        def fp8_pass(acc, m, j0):
+            h, c0 = divmod(m * P, HALF)
+            nc.tensor.matmul_mx(
+                out=acc[:],
+                lhsT=w8_codes[h][:, c0 : c0 + P].bitcast(FP8X4),
+                lhsT_scale=w8_plane[h][:, c0 : c0 + P],
+                rhs=picked0[:, j0 : j0 + BANK].bitcast(FP8X4),
+                rhs_scale=picked_scales[FP8_PLANE:P, j0 : j0 + BANK],
+                start=True,
+                stop=False,
+            )
+
+        def fp4_pass(acc, m, j0):
+            if j0 < FIRST:
+                moving = picked1_first[:, j0 : j0 + BANK]
+            else:
+                moving = picked1_rest[:, j0 - FIRST : j0 - FIRST + BANK]
+            nc.tensor.matmul_mx(
+                out=acc[:],
+                lhsT=w4_codes[:, 2 * m * P : 2 * (m + 1) * P].bitcast(FP4X4),
+                lhsT_scale=w4_plane[:, m * P : (m + 1) * P],
+                rhs=moving.bitcast(FP8X4),
+                rhs_scale=picked_scales[:, j0 : j0 + BANK],
+                start=False,
+                stop=True,
+            )
+
+        def piece(m, j0, j1):
+            values = keep.tile([P, j1 - j0], F32, name=f"values{m}_{j0}")
+            for j in range(j0, j1, BANK):
+                acc = psum.tile([P, BANK], F32, name="acc")
+                fp8_pass(acc, m, j)
+                fp4_pass(acc, m, j)
+                nc.scalar.activation(values[:, j - j0 : j - j0 + BANK], acc[:], GELU, bias=bias[:, m : m + 1])
+            window = windows[m % 2]
+            nc.vector.tensor_tensor(
+                window[:].indirect(list_slice(scatter_list, j0, j1)), values[:], weight[:, j0:j1], MULT
+            )
+            if j1 == S:
+                nc.sync.dma_start(out[m * P : (m + 1) * P, :], window[:])
+
+        piece(0, 0, FIRST)
+        piece(1, 0, FIRST)
+        piece(0, FIRST, S)
+        quantise_w8(1)
+        piece(1, FIRST, S)
+        piece(2, 0, S)
+        piece(3, 0, S)

@@ -62,19 +62,16 @@ def tile_list_tabscat_o_gelu_kernel(
         w4_plane = keep.tile([P, M], U8, name="w4_plane", align_bytes=64)
         bias = keep.tile([P, ROW_TILES], F32, name="bias")
         weight = keep.tile([P, S], F32, name="weight")
-        warm_in = keep.tile([P, 8], F32, name="warm_in")
         warm_out = keep.tile([P, 8], F32, name="warm_out")
         picked0 = keep.tile([P, S], U32, name="picked0", align_bytes=64)
         picked1_first = keep.tile([P, FIRST], U32, name="picked1_first", align_bytes=64)
         picked1_rest = keep.tile([P, S - FIRST], U32, name="picked1_rest", align_bytes=64)
         picked_scales = keep.tile([P, S], U8, name="picked_scales", align_bytes=64)
 
-        nc.gpsimd.memset(warm_in[:], 0.0)
-        nc.gpsimd.memset(w4_plane[:].bitcast(I32), 0)
         nc.scalar.dma_start(scale_window[100:P, :], scale_groups(3, 7))
-        nc.scalar.activation(warm_out[:], warm_in[:], GELU)
         for window in windows:
             nc.vector.memset(window[:], 0.0)
+        nc.scalar.activation(warm_out[:], windows[0][:, 0:8], GELU)
 
         w8_rows = w8.rearrange("(p j) n -> p j n", j=PACK)
         nc.sync.dma_start(gather_list[:], offs)
@@ -86,14 +83,17 @@ def tile_list_tabscat_o_gelu_kernel(
         nc.sync.dma_start(w8_raw[0][:], w8_rows[:, :, 0:HALF])
         nc.sync.dma_start(words[1][:], table_words(1))
         nc.sync.dma_start(w4_codes[:].bitcast(I32), w4_words.bitcast(I32)[0])
+        w4_scale_rows = w4_scales.bitcast(I32)[0]
+        for quadrant in range(4):
+            nc.sync.dma_start(
+                w4_plane[:].bitcast(I32)[32 * quadrant : 32 * (quadrant + 1), :],
+                w4_scale_rows[4 * quadrant : 4 * (quadrant + 1), :].partition_broadcast(8),
+            )
         with nc.allow_non_contiguous_dma(reason="one bias value a partition and row tile"):
             nc.sync.dma_start(bias[:], b.rearrange("(m p) -> p m", p=P))
         nc.sync.dma_start(scatter_list[:], offs2)
         nc.sync.dma_start(weight[:], wgo)
         nc.sync.dma_start(w8_raw[1][:], w8_rows[:, :, HALF:M])
-        w4_scale_rows = w4_scales.bitcast(I32)[0].rearrange("(q r) w -> r q w", r=4)
-        for r in range(4):
-            nc.gpsimd.dma_start(w4_plane[:].bitcast(I32)[r:P:32, :], w4_scale_rows[r])
 
         def quantise_w8(h):
             nc.scalar.copy(

@@ -1,6 +1,7 @@
 from contextlib import ExitStack
 
 import concourse.mybir as mybir
+from concourse.masks import make_identity
 
 K, M, T, S = 1024, 512, 4096, 2048
 FLOPS = 2 * K * M * S
@@ -35,7 +36,8 @@ def tile_list_tabscat_o_gelu_kernel(
     nc = tc.nc
     with ExitStack() as ctx:
         keep = ctx.enter_context(tc.tile_pool(name="keep", bufs=1))
-        psum = ctx.enter_context(tc.psum_pool(name="psum", bufs=8))
+        psum = ctx.enter_context(tc.psum_pool(name="psum", bufs=4))
+        psum_bias = ctx.enter_context(tc.psum_pool(name="psum_bias", bufs=1))
 
         tab32 = tab.bitcast(I32)
 
@@ -61,6 +63,8 @@ def tile_list_tabscat_o_gelu_kernel(
         w4_codes = keep.tile([P, 2 * M], U8, name="w4_codes", align_bytes=64)
         w4_plane = keep.tile([P, M], U8, name="w4_plane", align_bytes=64)
         bias = keep.tile([P, ROW_TILES], F32, name="bias")
+        bias_rows = keep.tile([P, P], F32, name="bias_rows")
+        identity = keep.tile([P, P], F32, name="identity")
         weight = keep.tile([P, S], F32, name="weight")
         warm_out = keep.tile([P, 8], F32, name="warm_out")
         picked0 = keep.tile([P, S], U32, name="picked0", align_bytes=64)
@@ -68,18 +72,23 @@ def tile_list_tabscat_o_gelu_kernel(
         picked1_rest = keep.tile([P, S - FIRST], U32, name="picked1_rest", align_bytes=64)
         picked_scales = keep.tile([P, S], U8, name="picked_scales", align_bytes=64)
 
-        nc.scalar.dma_start(scale_window[100:P, :], scale_groups(3, 7))
+        nc.gpsimd.memset(bias_rows[:], 0.0)
+        make_identity(nc, identity[:])
         for window in windows:
-            nc.vector.memset(window[:], 0.0)
+            nc.vector.memset(window[:].bitcast(I32), 0)
         nc.scalar.activation(warm_out[:], windows[0][:, 0:8], GELU)
 
         w8_rows = w8.rearrange("(p j) n -> p j n", j=PACK)
         nc.sync.dma_start(gather_list[:], offs)
-        nc.sync.dma_start(scale_window[0:4, :], tab_rows[PASS_ROWS + SCALE_ROW : PASS_ROWS + SCALE_ROW + 4, :])
         for quadrant in range(3):
             first = 32 * quadrant + FP8_PLANE
             nc.sync.dma_start(scale_window[first : first + 32, :], scale_groups(quadrant, 8))
+        nc.sync.dma_start(scale_window[0:4, :], tab_rows[PASS_ROWS + SCALE_ROW : PASS_ROWS + SCALE_ROW + 4, :])
+        nc.sync.dma_start(scale_window[100:104, :], tab_rows[SCALE_ROW + 12 : SCALE_ROW + 16, :])
+        nc.sync.dma_start(scale_window[104:112, :], tab_rows[SCALE_ROW : SCALE_ROW + 8, :])
+        nc.sync.dma_start(scale_window[112:128, :], tab_rows[SCALE_ROW : SCALE_ROW + 16, :])
         nc.sync.dma_start(words[0][:], table_words(0))
+        nc.sync.dma_start(bias_rows[0:ROW_TILES, :], b.rearrange("(m p) -> m p", p=P))
         nc.sync.dma_start(w8_raw[0][:], w8_rows[:, :, 0:HALF])
         nc.sync.dma_start(words[1][:], table_words(1))
         nc.sync.dma_start(w4_codes[:].bitcast(I32), w4_words.bitcast(I32)[0])
@@ -89,11 +98,14 @@ def tile_list_tabscat_o_gelu_kernel(
                 w4_plane[:].bitcast(I32)[32 * quadrant : 32 * (quadrant + 1), :],
                 w4_scale_rows[4 * quadrant : 4 * (quadrant + 1), :].partition_broadcast(8),
             )
-        with nc.allow_non_contiguous_dma(reason="one bias value a partition and row tile"):
-            nc.sync.dma_start(bias[:], b.rearrange("(m p) -> p m", p=P))
         nc.sync.dma_start(scatter_list[:], offs2)
-        nc.sync.dma_start(weight[:], wgo)
+        nc.sync.dma_start(weight[:, 0:FIRST], wgo[:, 0:FIRST])
         nc.sync.dma_start(w8_raw[1][:], w8_rows[:, :, HALF:M])
+        nc.sync.dma_start(weight[:, FIRST:S], wgo[:, FIRST:S])
+
+        bias_columns = psum_bias.tile([P, P], F32, name="bias_columns")
+        nc.tensor.transpose(bias_columns[:], bias_rows[:], identity[:])
+        nc.scalar.copy(bias[:], bias_columns[:, 0:ROW_TILES])
 
         def quantise_w8(h):
             nc.scalar.copy(

@@ -54,8 +54,8 @@ def tile_list_tabscat_o_gelu_kernel(
         gather_list = keep.tile([P, S // STRIPE], U16, name="gather_list")
         scatter_list = keep.tile([P, S // STRIPE], U16, name="scatter_list")
         words = [keep.tile([P, T], I32, name=f"words{a}", align_bytes=64) for a in range(2)]
-        scale_window = keep.tile([P, T // 4], I32, name="scale_window", align_bytes=64)
-        windows = [keep.tile([P, T], F32, name=f"window{i}", align_bytes=64) for i in range(2)]
+        scale_window = keep.tile([P, T // 4], I32, name="scale_window", tag="late_window", align_bytes=64)
+        windows = [keep.tile([P, T], F32, name="window0", align_bytes=64)]
         w8_raw = [keep.tile([P, PACK, HALF], F32, name=f"w8_raw{h}") for h in range(2)]
         w8_bf16 = [keep.tile([P, HALF, PACK], BF16, name=f"w8_bf16_{h}", align_bytes=64) for h in range(2)]
         w8_codes = [keep.tile([P, HALF], U32, name=f"w8_codes{h}", align_bytes=64) for h in range(2)]
@@ -74,8 +74,7 @@ def tile_list_tabscat_o_gelu_kernel(
 
         nc.gpsimd.memset(bias_rows[:], 0.0)
         make_identity(nc, identity[:])
-        for window in windows:
-            nc.vector.memset(window[:].bitcast(I32), 0)
+        nc.vector.memset(windows[0][:].bitcast(I32), 0)
         nc.scalar.activation(warm_out[:], windows[0][:, 0:8], GELU)
 
         w8_rows = w8.rearrange("(p j) n -> p j n", j=PACK)
@@ -122,6 +121,8 @@ def tile_list_tabscat_o_gelu_kernel(
             return offsets[:, j0 // STRIPE : j1 // STRIPE]
 
         nc.vector.tensor_copy(picked_scales[:], scale_window[:].bitcast(U8).indirect(gather_list[:]))
+        windows.append(keep.tile([P, T], F32, name="window1", tag="late_window", align_bytes=64))
+        nc.gpsimd.memset(windows[1][:].bitcast(I32), 0)
         nc.vector.tensor_copy(picked0[:], words[0][:].bitcast(U32).indirect(gather_list[:]))
         quantise_w8(0)
         nc.vector.tensor_copy(

@@ -24,10 +24,9 @@ STRIPE = 16
 ROW_TILES = M // P
 HALF = M // 2
 FIRST = 512
-FP8_PLANE = 4
-SCALE_ROW = 512
-PASS_ROWS = 528
-GROUP_STEP = (PASS_ROWS + 4) // 7
+EARLY = 1024
+SCALE_ROWS = 16
+SCALE_BASE = P - 2 * SCALE_ROWS
 
 
 def tile_list_tabscat_o_gelu_kernel(
@@ -36,7 +35,7 @@ def tile_list_tabscat_o_gelu_kernel(
     nc = tc.nc
     with ExitStack() as ctx:
         keep = ctx.enter_context(tc.tile_pool(name="keep", bufs=1))
-        psum = ctx.enter_context(tc.psum_pool(name="psum", bufs=4))
+        psum = ctx.enter_context(tc.psum_pool(name="psum", bufs=2))
         psum_bias = ctx.enter_context(tc.psum_pool(name="psum_bias", bufs=1))
 
         tab32 = tab.bitcast(I32)
@@ -44,20 +43,14 @@ def tile_list_tabscat_o_gelu_kernel(
         def table_words(a):
             return tab32[a, 0 : P * T].rearrange("(p t) -> p t", p=P)
 
-        tab_rows = tab32.rearrange("a (x w) -> (a x) w", w=T // 4)
-
-        def scale_groups(quadrant, groups):
-            first = SCALE_ROW + 4 * quadrant + 4 - GROUP_STEP
-            rows = tab_rows[first : first + GROUP_STEP * groups, :].rearrange("(u x) w -> u x w", u=groups)
-            return rows[:, GROUP_STEP - 4 :, :]
+        def table_scales(a):
+            return tab32[a, P * T : P * T + SCALE_ROWS * T // 4].rearrange("(q w) -> q w", q=SCALE_ROWS)
 
         gather_list = keep.tile([P, S // STRIPE], U16, name="gather_list")
         scatter_list = keep.tile([P, S // STRIPE], U16, name="scatter_list")
         words = [keep.tile([P, T], I32, name=f"words{a}", align_bytes=64) for a in range(2)]
         scale_window = keep.tile([P, T // 4], I32, name="scale_window", tag="late_window", align_bytes=64)
         windows = [keep.tile([P, T], F32, name="window0", align_bytes=64)]
-        w8_raw = [keep.tile([P, PACK, HALF], F32, name=f"w8_raw{h}") for h in range(2)]
-        w8_bf16 = [keep.tile([P, HALF, PACK], BF16, name=f"w8_bf16_{h}", align_bytes=64) for h in range(2)]
         w8_codes = [keep.tile([P, HALF], U32, name=f"w8_codes{h}", align_bytes=64) for h in range(2)]
         w8_plane = [keep.tile([P, HALF], U8, name=f"w8_plane{h}", align_bytes=64) for h in range(2)]
         w4_codes = keep.tile([P, 2 * M], U8, name="w4_codes", align_bytes=64)
@@ -65,72 +58,104 @@ def tile_list_tabscat_o_gelu_kernel(
         bias = keep.tile([P, ROW_TILES], F32, name="bias")
         bias_rows = keep.tile([P, P], F32, name="bias_rows")
         identity = keep.tile([P, P], F32, name="identity")
-        weight = keep.tile([P, S], F32, name="weight")
+        weight_first = keep.tile([P, FIRST], F32, name="weight_first")
         warm_out = keep.tile([P, 8], F32, name="warm_out")
         picked0 = keep.tile([P, S], U32, name="picked0", align_bytes=64)
-        picked1_first = keep.tile([P, FIRST], U32, name="picked1_first", align_bytes=64)
-        picked1_rest = keep.tile([P, S - FIRST], U32, name="picked1_rest", align_bytes=64)
-        picked_scales = keep.tile([P, S], U8, name="picked_scales", align_bytes=64)
+        picked1_early = keep.tile([P, EARLY], U32, name="picked1_early", align_bytes=64)
+        picked_scales = keep.tile([P, S], U8, name="picked_scales", tag="late_weight", align_bytes=64)
+        planes = [keep.tile([P, S], U8, name=f"plane{a}", align_bytes=64) for a in range(2)]
 
-        nc.gpsimd.memset(bias_rows[:], 0.0)
-        make_identity(nc, identity[:])
+        nc.vector.memset(scale_window[0:SCALE_BASE, :], 0)
         nc.vector.memset(windows[0][:].bitcast(I32), 0)
+        nc.vector.memset(bias_rows[:], 0.0)
+        nc.vector.memset(identity[:], 0.0)
+        make_identity(nc, identity[:], nomemset=True)
         nc.scalar.activation(warm_out[:], windows[0][:, 0:8], GELU)
 
         w8_rows = w8.rearrange("(p j) n -> p j n", j=PACK)
+
+        def load_w8(h):
+            raw = keep.tile([P, PACK, HALF], F32, name=f"w8_raw{h}", tag="w8_raw")
+            nc.sync.dma_start(raw[:], w8_rows[:, :, h * HALF : (h + 1) * HALF])
+            return raw
+
         nc.sync.dma_start(gather_list[:], offs)
-        for quadrant in range(3):
-            first = 32 * quadrant + FP8_PLANE
-            nc.sync.dma_start(scale_window[first : first + 32, :], scale_groups(quadrant, 8))
-        nc.sync.dma_start(scale_window[0:4, :], tab_rows[PASS_ROWS + SCALE_ROW : PASS_ROWS + SCALE_ROW + 4, :])
-        nc.sync.dma_start(scale_window[100:104, :], tab_rows[SCALE_ROW + 12 : SCALE_ROW + 16, :])
-        nc.sync.dma_start(scale_window[104:112, :], tab_rows[SCALE_ROW : SCALE_ROW + 8, :])
-        nc.sync.dma_start(scale_window[112:128, :], tab_rows[SCALE_ROW : SCALE_ROW + 16, :])
+        for a in range(2):
+            first = SCALE_BASE + a * SCALE_ROWS
+            nc.sync.dma_start(scale_window[first : first + SCALE_ROWS, :], table_scales(a))
         nc.sync.dma_start(words[0][:], table_words(0))
-        nc.sync.dma_start(bias_rows[0:ROW_TILES, :], b.rearrange("(m p) -> m p", p=P))
-        nc.sync.dma_start(w8_raw[0][:], w8_rows[:, :, 0:HALF])
         nc.sync.dma_start(words[1][:], table_words(1))
+        w8_raw0 = load_w8(0)
         nc.sync.dma_start(w4_codes[:].bitcast(I32), w4_words.bitcast(I32)[0])
+        nc.sync.dma_start(scatter_list[:], offs2)
+        nc.sync.dma_start(weight_first[:], wgo[:, 0:FIRST])
         w4_scale_rows = w4_scales.bitcast(I32)[0]
         for quadrant in range(4):
-            nc.sync.dma_start(
-                w4_plane[:].bitcast(I32)[32 * quadrant : 32 * (quadrant + 1), :],
-                w4_scale_rows[4 * quadrant : 4 * (quadrant + 1), :].partition_broadcast(8),
+            nc.gpsimd.dma_start(
+                w4_plane[:].bitcast(I32)[32 * quadrant : 32 * quadrant + 4, :],
+                w4_scale_rows[4 * quadrant : 4 * (quadrant + 1), :],
             )
-        nc.sync.dma_start(scatter_list[:], offs2)
-        nc.sync.dma_start(weight[:, 0:FIRST], wgo[:, 0:FIRST])
-        nc.sync.dma_start(w8_raw[1][:], w8_rows[:, :, HALF:M])
-        nc.sync.dma_start(weight[:, FIRST:S], wgo[:, FIRST:S])
+        nc.gpsimd.dma_start(bias_rows[0:ROW_TILES, :], b.rearrange("(m p) -> m p", p=P))
 
         bias_columns = psum_bias.tile([P, P], F32, name="bias_columns")
         nc.tensor.transpose(bias_columns[:], bias_rows[:], identity[:])
         nc.scalar.copy(bias[:], bias_columns[:, 0:ROW_TILES])
 
-        def quantise_w8(h):
+        def quantise_w8(h, raw, tag):
+            rounded = keep.tile([P, HALF, PACK], BF16, name=f"w8_bf16_{h}", tag=tag, align_bytes=64)
             nc.scalar.copy(
-                w8_bf16[h][:].rearrange("p (c i) j -> p c j i", i=4),
-                w8_raw[h][:].rearrange("p j (c i) -> p c j i", i=4),
+                rounded[:].rearrange("p (c i) j -> p c j i", i=4),
+                raw[:].rearrange("p j (c i) -> p c j i", i=4),
             )
             nc.vector.quantize_mx(
                 out=w8_codes[h][:].bitcast(FP8X4),
                 scales=w8_plane[h][:],
-                in_=w8_bf16[h][:].rearrange("p n j -> p (n j)"),
+                in_=rounded[:].rearrange("p n j -> p (n j)"),
             )
 
         def list_slice(offsets, j0, j1):
             return offsets[:, j0 // STRIPE : j1 // STRIPE]
 
         nc.vector.tensor_copy(picked_scales[:], scale_window[:].bitcast(U8).indirect(gather_list[:]))
+        for a in (1, 0):
+            for quadrant in range(4):
+                first = SCALE_BASE + a * SCALE_ROWS + 4 * quadrant
+                nc.sync.dma_start(
+                    planes[a][:].bitcast(I32)[32 * quadrant : 32 * quadrant + 4, :],
+                    picked_scales[:].bitcast(I32)[first : first + 4, :],
+                )
         windows.append(keep.tile([P, T], F32, name="window1", tag="late_window", align_bytes=64))
         nc.gpsimd.memset(windows[1][:].bitcast(I32), 0)
+        weight_all = keep.tile([P, S], F32, name="weight_all", tag="late_weight", align_bytes=64)
+        nc.sync.dma_start(weight_all[:], wgo)
+
         nc.vector.tensor_copy(picked0[:], words[0][:].bitcast(U32).indirect(gather_list[:]))
-        quantise_w8(0)
+        for j0 in range(0, EARLY, BANK):
+            nc.vector.tensor_copy(
+                picked1_early[:, j0 : j0 + BANK],
+                words[1][:].bitcast(U32).indirect(list_slice(gather_list, j0, j0 + BANK)),
+            )
+        quantise_w8(0, w8_raw0, "late_picked")
+        picked1_late = keep.tile([P, S - EARLY], U32, name="picked1_late", tag="late_picked", align_bytes=64)
         nc.vector.tensor_copy(
-            picked1_first[:], words[1][:].bitcast(U32).indirect(list_slice(gather_list, 0, FIRST))
+            picked1_late[:], words[1][:].bitcast(U32).indirect(list_slice(gather_list, EARLY, S))
         )
-        nc.vector.tensor_copy(
-            picked1_rest[:], words[1][:].bitcast(U32).indirect(list_slice(gather_list, FIRST, S))
-        )
+        w8_raw1 = load_w8(1)
+
+        def fp4_pass(acc, m, j0):
+            if j0 < EARLY:
+                moving = picked1_early[:, j0 : j0 + BANK]
+            else:
+                moving = picked1_late[:, j0 - EARLY : j0 - EARLY + BANK]
+            nc.tensor.matmul_mx(
+                out=acc[:],
+                lhsT=w4_codes[:, 2 * m * P : 2 * (m + 1) * P].bitcast(FP4X4),
+                lhsT_scale=w4_plane[:, m * P : (m + 1) * P],
+                rhs=moving.bitcast(FP8X4),
+                rhs_scale=planes[1][:, j0 : j0 + BANK],
+                start=True,
+                stop=False,
+            )
 
         def fp8_pass(acc, m, j0):
             h, c0 = divmod(m * P, HALF)
@@ -139,34 +164,20 @@ def tile_list_tabscat_o_gelu_kernel(
                 lhsT=w8_codes[h][:, c0 : c0 + P].bitcast(FP8X4),
                 lhsT_scale=w8_plane[h][:, c0 : c0 + P],
                 rhs=picked0[:, j0 : j0 + BANK].bitcast(FP8X4),
-                rhs_scale=picked_scales[FP8_PLANE:P, j0 : j0 + BANK],
-                start=True,
-                stop=False,
-            )
-
-        def fp4_pass(acc, m, j0):
-            if j0 < FIRST:
-                moving = picked1_first[:, j0 : j0 + BANK]
-            else:
-                moving = picked1_rest[:, j0 - FIRST : j0 - FIRST + BANK]
-            nc.tensor.matmul_mx(
-                out=acc[:],
-                lhsT=w4_codes[:, 2 * m * P : 2 * (m + 1) * P].bitcast(FP4X4),
-                lhsT_scale=w4_plane[:, m * P : (m + 1) * P],
-                rhs=moving.bitcast(FP8X4),
-                rhs_scale=picked_scales[:, j0 : j0 + BANK],
+                rhs_scale=planes[0][:, j0 : j0 + BANK],
                 start=False,
                 stop=True,
             )
 
         def piece(m, j0, j1):
-            values = keep.tile([P, j1 - j0], F32, name=f"values{m}_{j0}")
+            values = keep.tile([P, j1 - j0], F32, name=f"values{m}_{j0}", tag=f"values{m}_{j0}", align_bytes=64)
             for j in range(j0, j1, BANK):
                 acc = psum.tile([P, BANK], F32, name="acc")
-                fp8_pass(acc, m, j)
                 fp4_pass(acc, m, j)
+                fp8_pass(acc, m, j)
                 nc.scalar.activation(values[:, j - j0 : j - j0 + BANK], acc[:], GELU, bias=bias[:, m : m + 1])
             window = windows[m % 2]
+            weight = weight_first if j1 == FIRST else weight_all
             nc.vector.tensor_tensor(
                 window[:].indirect(list_slice(scatter_list, j0, j1)), values[:], weight[:, j0:j1], MULT
             )
@@ -175,8 +186,8 @@ def tile_list_tabscat_o_gelu_kernel(
 
         piece(0, 0, FIRST)
         piece(1, 0, FIRST)
+        quantise_w8(1, w8_raw1, "values0_0")
         piece(0, FIRST, S)
-        quantise_w8(1)
         piece(1, FIRST, S)
         piece(2, 0, S)
         piece(3, 0, S)

@@ -27,6 +27,7 @@ FIRST = 512
 EARLY = 1024
 SCALE_ROWS = 16
 SCALE_BASE = P - 2 * SCALE_ROWS
+VECTOR_ZEROS = 3 * T // 4
 
 
 def tile_list_tabscat_o_gelu_kernel(
@@ -48,9 +49,9 @@ def tile_list_tabscat_o_gelu_kernel(
 
         gather_list = keep.tile([P, S // STRIPE], U16, name="gather_list")
         scatter_list = keep.tile([P, S // STRIPE], U16, name="scatter_list")
-        words = [keep.tile([P, T], I32, name=f"words{a}", align_bytes=64) for a in range(2)]
-        scale_window = keep.tile([P, T // 4], I32, name="scale_window", tag="late_window", align_bytes=64)
-        windows = [keep.tile([P, T], F32, name="window0", align_bytes=64)]
+        words = [keep.tile([P, T], I32, name=f"words{a}", tag=f"words{a}", align_bytes=64) for a in range(2)]
+        scale_window = keep.tile([P, T // 4], I32, name="scale_window", align_bytes=64)
+        windows = [keep.tile([P, T], F32, name=f"window{i}", align_bytes=64) for i in range(2)]
         w8_codes = [keep.tile([P, HALF], U32, name=f"w8_codes{h}", align_bytes=64) for h in range(2)]
         w8_plane = [keep.tile([P, HALF], U8, name=f"w8_plane{h}", align_bytes=64) for h in range(2)]
         w4_codes = keep.tile([P, 2 * M], U8, name="w4_codes", align_bytes=64)
@@ -58,18 +59,14 @@ def tile_list_tabscat_o_gelu_kernel(
         bias = keep.tile([P, ROW_TILES], F32, name="bias")
         bias_rows = keep.tile([P, P], F32, name="bias_rows")
         identity = keep.tile([P, P], F32, name="identity")
-        weight_first = keep.tile([P, FIRST], F32, name="weight_first")
         warm_out = keep.tile([P, 8], F32, name="warm_out")
         picked0 = keep.tile([P, S], U32, name="picked0", align_bytes=64)
         picked1_early = keep.tile([P, EARLY], U32, name="picked1_early", align_bytes=64)
-        picked_scales = keep.tile([P, S], U8, name="picked_scales", tag="late_weight", align_bytes=64)
+        picked_scales = keep.tile([P, S], U8, name="picked_scales", align_bytes=64)
         planes = [keep.tile([P, S], U8, name=f"plane{a}", align_bytes=64) for a in range(2)]
 
         nc.vector.memset(scale_window[0:SCALE_BASE, :], 0)
-        nc.vector.memset(windows[0][:].bitcast(I32), 0)
-        nc.vector.memset(bias_rows[:], 0.0)
-        nc.vector.memset(identity[:], 0.0)
-        make_identity(nc, identity[:], nomemset=True)
+        nc.vector.memset(windows[0][:, 0:VECTOR_ZEROS].bitcast(I32), 0)
         nc.scalar.activation(warm_out[:], windows[0][:, 0:8], GELU)
 
         w8_rows = w8.rearrange("(p j) n -> p j n", j=PACK)
@@ -81,21 +78,23 @@ def tile_list_tabscat_o_gelu_kernel(
 
         nc.sync.dma_start(gather_list[:], offs)
         for a in range(2):
-            first = SCALE_BASE + a * SCALE_ROWS
-            nc.sync.dma_start(scale_window[first : first + SCALE_ROWS, :], table_scales(a))
+            nc.sync.dma_start(scale_window[SCALE_BASE + a : P : 2, :], table_scales(a))
         nc.sync.dma_start(words[0][:], table_words(0))
         nc.sync.dma_start(words[1][:], table_words(1))
         w8_raw0 = load_w8(0)
         nc.sync.dma_start(w4_codes[:].bitcast(I32), w4_words.bitcast(I32)[0])
         nc.sync.dma_start(scatter_list[:], offs2)
-        nc.sync.dma_start(weight_first[:], wgo[:, 0:FIRST])
         w4_scale_rows = w4_scales.bitcast(I32)[0]
         for quadrant in range(4):
             nc.gpsimd.dma_start(
                 w4_plane[:].bitcast(I32)[32 * quadrant : 32 * quadrant + 4, :],
                 w4_scale_rows[4 * quadrant : 4 * (quadrant + 1), :],
             )
+        nc.gpsimd.memset(bias_rows[:], 0.0)
         nc.gpsimd.dma_start(bias_rows[0:ROW_TILES, :], b.rearrange("(m p) -> m p", p=P))
+        make_identity(nc, identity[:])
+        nc.gpsimd.memset(windows[0][:, VECTOR_ZEROS:T].bitcast(I32), 0)
+        nc.gpsimd.memset(windows[1][:].bitcast(I32), 0)
 
         bias_columns = psum_bias.tile([P, P], F32, name="bias_columns")
         nc.tensor.transpose(bias_columns[:], bias_rows[:], identity[:])
@@ -119,17 +118,16 @@ def tile_list_tabscat_o_gelu_kernel(
         nc.vector.tensor_copy(picked_scales[:], scale_window[:].bitcast(U8).indirect(gather_list[:]))
         for a in (1, 0):
             for quadrant in range(4):
-                first = SCALE_BASE + a * SCALE_ROWS + 4 * quadrant
+                first = SCALE_BASE + a + 8 * quadrant
                 nc.sync.dma_start(
                     planes[a][:].bitcast(I32)[32 * quadrant : 32 * quadrant + 4, :],
-                    picked_scales[:].bitcast(I32)[first : first + 4, :],
+                    picked_scales[:].bitcast(I32)[first : first + 7 : 2, :],
                 )
-        windows.append(keep.tile([P, T], F32, name="window1", tag="late_window", align_bytes=64))
-        nc.gpsimd.memset(windows[1][:].bitcast(I32), 0)
-        weight_all = keep.tile([P, S], F32, name="weight_all", tag="late_weight", align_bytes=64)
-        nc.sync.dma_start(weight_all[:], wgo)
 
         nc.vector.tensor_copy(picked0[:], words[0][:].bitcast(U32).indirect(gather_list[:]))
+        weight = keep.tile([P, S], F32, name="weight", tag="words0", align_bytes=64)
+        nc.sync.dma_start(weight[:, 0:FIRST], wgo[:, 0:FIRST])
+        nc.sync.dma_start(weight[:, FIRST:S], wgo[:, FIRST:S])
         for j0 in range(0, EARLY, BANK):
             nc.vector.tensor_copy(
                 picked1_early[:, j0 : j0 + BANK],
@@ -177,7 +175,6 @@ def tile_list_tabscat_o_gelu_kernel(
                 fp8_pass(acc, m, j)
                 nc.scalar.activation(values[:, j - j0 : j - j0 + BANK], acc[:], GELU, bias=bias[:, m : m + 1])
             window = windows[m % 2]
-            weight = weight_first if j1 == FIRST else weight_all
             nc.vector.tensor_tensor(
                 window[:].indirect(list_slice(scatter_list, j0, j1)), values[:], weight[:, j0:j1], MULT
             )

@@ -71,8 +71,8 @@ def tile_list_tabscat_o_gelu_kernel(
 
         w8_rows = w8.rearrange("(p j) n -> p j n", j=PACK)
 
-        def load_w8(h):
-            raw = keep.tile([P, PACK, HALF], F32, name=f"w8_raw{h}", tag="w8_raw")
+        def load_w8(h, tag):
+            raw = keep.tile([P, PACK, HALF], F32, name=f"w8_raw{h}", tag=tag, align_bytes=64)
             nc.sync.dma_start(raw[:], w8_rows[:, :, h * HALF : (h + 1) * HALF])
             return raw
 
@@ -81,7 +81,7 @@ def tile_list_tabscat_o_gelu_kernel(
             nc.sync.dma_start(scale_window[SCALE_BASE + a : P : 2, :], table_scales(a))
         nc.sync.dma_start(words[0][:], table_words(0))
         nc.sync.dma_start(words[1][:], table_words(1))
-        w8_raw0 = load_w8(0)
+        w8_raw0 = load_w8(0, "late_picked")
         nc.sync.dma_start(w4_codes[:].bitcast(I32), w4_words.bitcast(I32)[0])
         nc.sync.dma_start(scatter_list[:], offs2)
         w4_scale_rows = w4_scales.bitcast(I32)[0]
@@ -133,12 +133,12 @@ def tile_list_tabscat_o_gelu_kernel(
                 picked1_early[:, j0 : j0 + BANK],
                 words[1][:].bitcast(U32).indirect(list_slice(gather_list, j0, j0 + BANK)),
             )
-        quantise_w8(0, w8_raw0, "late_picked")
+        quantise_w8(0, w8_raw0, "late_w8")
         picked1_late = keep.tile([P, S - EARLY], U32, name="picked1_late", tag="late_picked", align_bytes=64)
         nc.vector.tensor_copy(
             picked1_late[:], words[1][:].bitcast(U32).indirect(list_slice(gather_list, EARLY, S))
         )
-        w8_raw1 = load_w8(1)
+        w8_raw1 = load_w8(1, "late_w8")
 
         def fp4_pass(acc, m, j0):
             if j0 < EARLY:
@@ -178,8 +178,11 @@ def tile_list_tabscat_o_gelu_kernel(
             nc.vector.tensor_tensor(
                 window[:].indirect(list_slice(scatter_list, j0, j1)), values[:], weight[:, j0:j1], MULT
             )
-            if j1 == S:
+            if j1 == S and m < ROW_TILES - 1:
                 nc.sync.dma_start(out[m * P : (m + 1) * P, :], window[:])
+            elif j1 == S:
+                nc.sync.dma_start(out[m * P : (m + 1) * P, 0 : T // 2], window[:, 0 : T // 2])
+                nc.scalar.dma_start(out[m * P : (m + 1) * P, T // 2 : T], window[:, T // 2 : T])
 
         piece(0, 0, FIRST)
         piece(1, 0, FIRST)

@@ -59,7 +59,6 @@ def tile_list_tabscat_o_gelu_kernel(
         bias = keep.tile([P, ROW_TILES], F32, name="bias")
         bias_rows = keep.tile([P, P], F32, name="bias_rows")
         identity = keep.tile([P, P], F32, name="identity")
-        warm_out = keep.tile([P, 8], F32, name="warm_out")
         picked0 = keep.tile([P, S], U32, name="picked0", align_bytes=64)
         picked1_early = keep.tile([P, EARLY], U32, name="picked1_early", align_bytes=64)
         picked_scales = keep.tile([P, S], U8, name="picked_scales", align_bytes=64)
@@ -67,7 +66,6 @@ def tile_list_tabscat_o_gelu_kernel(
 
         nc.vector.memset(scale_window[0:SCALE_BASE, :], 0)
         nc.vector.memset(windows[0][:, 0:VECTOR_ZEROS].bitcast(I32), 0)
-        nc.scalar.activation(warm_out[:], windows[0][:, 0:8], GELU)
 
         w8_rows = w8.rearrange("(p j) n -> p j n", j=PACK)
 

@@ -176,11 +176,8 @@ def tile_list_tabscat_o_gelu_kernel(
             nc.vector.tensor_tensor(
                 window[:].indirect(list_slice(scatter_list, j0, j1)), values[:], weight[:, j0:j1], MULT
             )
-            if j1 == S and m < ROW_TILES - 1:
+            if j1 == S:
                 nc.sync.dma_start(out[m * P : (m + 1) * P, :], window[:])
-            elif j1 == S:
-                nc.sync.dma_start(out[m * P : (m + 1) * P, 0 : T // 2], window[:, 0 : T // 2])
-                nc.scalar.dma_start(out[m * P : (m + 1) * P, T // 2 : T], window[:, T // 2 : T])
 
         piece(0, 0, FIRST)
         piece(1, 0, FIRST)

@@ -27,7 +27,7 @@ FIRST = 512
 EARLY = 1024
 SCALE_ROWS = 16
 SCALE_BASE = P - 2 * SCALE_ROWS
-VECTOR_ZEROS = 3 * T // 4
+VECTOR_ZEROS = T // 2
 
 
 def tile_list_tabscat_o_gelu_kernel(
@@ -43,9 +43,6 @@ def tile_list_tabscat_o_gelu_kernel(
 
         def table_words(a):
             return tab32[a, 0 : P * T].rearrange("(p t) -> p t", p=P)
-
-        def table_scales(a):
-            return tab32[a, P * T : P * T + SCALE_ROWS * T // 4].rearrange("(q w) -> q w", q=SCALE_ROWS)
 
         gather_list = keep.tile([P, S // STRIPE], U16, name="gather_list")
         scatter_list = keep.tile([P, S // STRIPE], U16, name="scatter_list")
@@ -74,9 +71,9 @@ def tile_list_tabscat_o_gelu_kernel(
             nc.sync.dma_start(raw[:], w8_rows[:, :, h * HALF : (h + 1) * HALF])
             return raw
 
+        scale_rows = tab32[:, P * T : P * T + SCALE_ROWS * T // 4].rearrange("a (q w) -> q a w", q=SCALE_ROWS)
+        nc.sync.dma_start(scale_window[SCALE_BASE:P, :], scale_rows)
         nc.sync.dma_start(gather_list[:], offs)
-        for a in range(2):
-            nc.sync.dma_start(scale_window[SCALE_BASE + a : P : 2, :], table_scales(a))
         nc.sync.dma_start(words[0][:], table_words(0))
         nc.sync.dma_start(words[1][:], table_words(1))
         w8_raw0 = load_w8(0, "late_picked")

@@ -112,11 +112,10 @@ def tile_list_tabscat_o_gelu_kernel(
 
         nc.vector.tensor_copy(picked_scales[:], scale_window[:].bitcast(U8).indirect(gather_list[:]))
         for a in (1, 0):
-            for quadrant in range(4):
-                first = SCALE_BASE + a + 8 * quadrant
+            for r in range(4):
                 nc.sync.dma_start(
-                    planes[a][:].bitcast(I32)[32 * quadrant : 32 * quadrant + 4, :],
-                    picked_scales[:].bitcast(I32)[first : first + 7 : 2, :],
+                    planes[a][:].bitcast(I32)[r:P:32, :],
+                    picked_scales[:].bitcast(I32)[SCALE_BASE + a + 2 * r : P : 8, :],
                 )
 
         nc.vector.tensor_copy(picked0[:], words[0][:].bitcast(U32).indirect(gather_list[:]))

@@ -59,7 +59,8 @@ def tile_list_tabscat_o_gelu_kernel(
         picked0 = keep.tile([P, S], U32, name="picked0", align_bytes=64)
         picked1_early = keep.tile([P, EARLY], U32, name="picked1_early", align_bytes=64)
         picked_scales = keep.tile([P, S], U8, name="picked_scales", align_bytes=64)
-        planes = [keep.tile([P, S], U8, name=f"plane{a}", align_bytes=64) for a in range(2)]
+        planes_first = keep.tile([P, 2 * FIRST], U8, name="planes_first", align_bytes=64)
+        planes_rest = keep.tile([P, 2 * (S - FIRST)], U8, name="planes_rest", align_bytes=64)
 
         nc.vector.memset(scale_window[0:SCALE_BASE, :], 0)
         nc.vector.memset(windows[0][:, 0:VECTOR_ZEROS].bitcast(I32), 0)
@@ -111,12 +112,23 @@ def tile_list_tabscat_o_gelu_kernel(
             return offsets[:, j0 // STRIPE : j1 // STRIPE]
 
         nc.vector.tensor_copy(picked_scales[:], scale_window[:].bitcast(U8).indirect(gather_list[:]))
-        for a in (1, 0):
-            for r in range(4):
+
+        def move_scales(planes, j0, j1):
+            for quadrant in (0, 2, 1, 3):
+                rows = slice(SCALE_BASE + 8 * quadrant, SCALE_BASE + 8 * (quadrant + 1))
                 nc.sync.dma_start(
-                    planes[a][:].bitcast(I32)[r:P:32, :],
-                    picked_scales[:].bitcast(I32)[SCALE_BASE + a + 2 * r : P : 8, :],
+                    planes[:].bitcast(I32)[32 * quadrant : 32 * quadrant + 4, :].rearrange("p (a w) -> p a w", a=2),
+                    picked_scales[:].bitcast(I32)[rows, j0 // 4 : j1 // 4],
                 )
+
+        def plane(a, j0):
+            if j0 < FIRST:
+                return planes_first[:, a * FIRST + j0 : a * FIRST + j0 + BANK]
+            c0 = a * (S - FIRST) + j0 - FIRST
+            return planes_rest[:, c0 : c0 + BANK]
+
+        move_scales(planes_first, 0, FIRST)
+        move_scales(planes_rest, FIRST, S)
 
         nc.vector.tensor_copy(picked0[:], words[0][:].bitcast(U32).indirect(gather_list[:]))
         weight = keep.tile([P, S], F32, name="weight", tag="words0", align_bytes=64)
@@ -144,7 +156,7 @@ def tile_list_tabscat_o_gelu_kernel(
                 lhsT=w4_codes[:, 2 * m * P : 2 * (m + 1) * P].bitcast(FP4X4),
                 lhsT_scale=w4_plane[:, m * P : (m + 1) * P],
                 rhs=moving.bitcast(FP8X4),
-                rhs_scale=planes[1][:, j0 : j0 + BANK],
+                rhs_scale=plane(1, j0),
                 start=True,
                 stop=False,
             )
@@ -156,7 +168,7 @@ def tile_list_tabscat_o_gelu_kernel(
                 lhsT=w8_codes[h][:, c0 : c0 + P].bitcast(FP8X4),
                 lhsT_scale=w8_plane[h][:, c0 : c0 + P],
                 rhs=picked0[:, j0 : j0 + BANK].bitcast(FP8X4),
-                rhs_scale=planes[0][:, j0 : j0 + BANK],
+                rhs_scale=plane(0, j0),
                 start=False,
                 stop=True,
             )

@@ -27,7 +27,6 @@ FIRST = 512
 EARLY = 1024
 SCALE_ROWS = 16
 SCALE_BASE = P - 2 * SCALE_ROWS
-VECTOR_ZEROS = T // 2
 
 
 def tile_list_tabscat_o_gelu_kernel(
@@ -62,8 +61,7 @@ def tile_list_tabscat_o_gelu_kernel(
         planes_first = keep.tile([P, 2 * FIRST], U8, name="planes_first", align_bytes=64)
         planes_rest = keep.tile([P, 2 * (S - FIRST)], U8, name="planes_rest", align_bytes=64)
 
-        nc.vector.memset(scale_window[0:SCALE_BASE, :], 0)
-        nc.vector.memset(windows[0][:, 0:VECTOR_ZEROS].bitcast(I32), 0)
+        nc.gpsimd.memset(scale_window[0:SCALE_BASE, :], 0)
 
         w8_rows = w8.rearrange("(p j) n -> p j n", j=PACK)
 
@@ -77,20 +75,20 @@ def tile_list_tabscat_o_gelu_kernel(
         nc.sync.dma_start(gather_list[:], offs)
         nc.sync.dma_start(words[0][:], table_words(0))
         nc.sync.dma_start(words[1][:], table_words(1))
-        w8_raw0 = load_w8(0, "late_picked")
-        nc.sync.dma_start(w4_codes[:].bitcast(I32), w4_words.bitcast(I32)[0])
-        nc.sync.dma_start(scatter_list[:], offs2)
+        nc.gpsimd.memset(bias_rows[:], 0.0)
+        nc.sync.dma_start(bias_rows[0:ROW_TILES, :], b.rearrange("(m p) -> m p", p=P))
         w4_scale_rows = w4_scales.bitcast(I32)[0]
-        for quadrant in range(4):
-            nc.gpsimd.dma_start(
+        for quadrant in (0, 2, 1, 3):
+            nc.sync.dma_start(
                 w4_plane[:].bitcast(I32)[32 * quadrant : 32 * quadrant + 4, :],
                 w4_scale_rows[4 * quadrant : 4 * (quadrant + 1), :],
             )
-        nc.gpsimd.memset(bias_rows[:], 0.0)
-        nc.gpsimd.dma_start(bias_rows[0:ROW_TILES, :], b.rearrange("(m p) -> m p", p=P))
+        w8_raw0 = load_w8(0, "late_picked")
+        nc.sync.dma_start(w4_codes[:].bitcast(I32), w4_words.bitcast(I32)[0])
+        nc.sync.dma_start(scatter_list[:], offs2)
         make_identity(nc, identity[:])
-        nc.gpsimd.memset(windows[0][:, VECTOR_ZEROS:T].bitcast(I32), 0)
-        nc.gpsimd.memset(windows[1][:].bitcast(I32), 0)
+        for window in windows:
+            nc.gpsimd.memset(window[:].bitcast(I32), 0)
 
         bias_columns = psum_bias.tile([P, P], F32, name="bias_columns")
         nc.tensor.transpose(bias_columns[:], bias_rows[:], identity[:])

@@ -58,8 +58,7 @@ def tile_list_tabscat_o_gelu_kernel(
         picked0 = keep.tile([P, S], U32, name="picked0", align_bytes=64)
         picked1_early = keep.tile([P, EARLY], U32, name="picked1_early", align_bytes=64)
         picked_scales = keep.tile([P, S], U8, name="picked_scales", align_bytes=64)
-        planes_first = keep.tile([P, 2 * FIRST], U8, name="planes_first", align_bytes=64)
-        planes_rest = keep.tile([P, 2 * (S - FIRST)], U8, name="planes_rest", align_bytes=64)
+        planes = keep.tile([P, 2 * S], U8, name="planes", align_bytes=64)
 
         nc.gpsimd.memset(scale_window[0:SCALE_BASE, :], 0)
 
@@ -110,23 +109,15 @@ def tile_list_tabscat_o_gelu_kernel(
             return offsets[:, j0 // STRIPE : j1 // STRIPE]
 
         nc.vector.tensor_copy(picked_scales[:], scale_window[:].bitcast(U8).indirect(gather_list[:]))
-
-        def move_scales(planes, j0, j1):
-            for quadrant in (0, 2, 1, 3):
-                rows = slice(SCALE_BASE + 8 * quadrant, SCALE_BASE + 8 * (quadrant + 1))
-                nc.sync.dma_start(
-                    planes[:].bitcast(I32)[32 * quadrant : 32 * quadrant + 4, :].rearrange("p (a w) -> p a w", a=2),
-                    picked_scales[:].bitcast(I32)[rows, j0 // 4 : j1 // 4],
-                )
+        for quadrant in (0, 2, 1, 3):
+            nc.sync.dma_start(
+                planes[:].bitcast(I32)[32 * quadrant : 32 * quadrant + 4, :].rearrange("p (a w) -> p a w", a=2),
+                picked_scales[:].bitcast(I32)[SCALE_BASE + 8 * quadrant : SCALE_BASE + 8 * (quadrant + 1), :],
+            )
 
         def plane(a, j0):
-            if j0 < FIRST:
-                return planes_first[:, a * FIRST + j0 : a * FIRST + j0 + BANK]
-            c0 = a * (S - FIRST) + j0 - FIRST
-            return planes_rest[:, c0 : c0 + BANK]
+            return planes[:, a * S + j0 : a * S + j0 + BANK]
 
-        move_scales(planes_first, 0, FIRST)
-        move_scales(planes_rest, FIRST, S)
 
         nc.vector.tensor_copy(picked0[:], words[0][:].bitcast(U32).indirect(gather_list[:]))
         weight = keep.tile([P, S], F32, name="weight", tag="words0", align_bytes=64)

@@ -23,10 +23,10 @@ BANK = 512
 STRIPE = 16
 ROW_TILES = M // P
 HALF = M // 2
-FIRST = 512
 EARLY = 1024
 SCALE_ROWS = 16
 SCALE_BASE = P - 2 * SCALE_ROWS
+QUADRANT_ORDER = (0, 2, 1, 3)
 
 
 def tile_list_tabscat_o_gelu_kernel(
@@ -38,53 +38,68 @@ def tile_list_tabscat_o_gelu_kernel(
         psum = ctx.enter_context(tc.psum_pool(name="psum", bufs=2))
         psum_bias = ctx.enter_context(tc.psum_pool(name="psum_bias", bufs=1))
 
+        def sbuf(name, shape, dtype, tag=None):
+            return keep.tile(shape, dtype, name=name, tag=tag or name, align_bytes=64)
+
         tab32 = tab.bitcast(I32)
-
-        def table_words(a):
-            return tab32[a, 0 : P * T].rearrange("(p t) -> p t", p=P)
-
         gather_list = keep.tile([P, S // STRIPE], U16, name="gather_list")
         scatter_list = keep.tile([P, S // STRIPE], U16, name="scatter_list")
-        words = [keep.tile([P, T], I32, name=f"words{a}", tag=f"words{a}", align_bytes=64) for a in range(2)]
-        scale_window = keep.tile([P, T // 4], I32, name="scale_window", align_bytes=64)
-        windows = [keep.tile([P, T], F32, name=f"window{i}", align_bytes=64) for i in range(2)]
-        w8_codes = [keep.tile([P, HALF], U32, name=f"w8_codes{h}", align_bytes=64) for h in range(2)]
-        w8_plane = [keep.tile([P, HALF], U8, name=f"w8_plane{h}", align_bytes=64) for h in range(2)]
-        w4_codes = keep.tile([P, 2 * M], U8, name="w4_codes", align_bytes=64)
-        w4_plane = keep.tile([P, M], U8, name="w4_plane", align_bytes=64)
-        bias = keep.tile([P, ROW_TILES], F32, name="bias")
-        bias_rows = keep.tile([P, P], F32, name="bias_rows")
-        identity = keep.tile([P, P], F32, name="identity")
-        picked0 = keep.tile([P, S], U32, name="picked0", align_bytes=64)
-        picked1_early = keep.tile([P, EARLY], U32, name="picked1_early", align_bytes=64)
-        picked_scales = keep.tile([P, S], U8, name="picked_scales", align_bytes=64)
-        planes = keep.tile([P, 2 * S], U8, name="planes", align_bytes=64)
+        words = [sbuf(f"words{a}", [P, T], I32) for a in range(2)]
+        scale_window = sbuf("scale_window", [P, T // 4], I32)
+        windows = [sbuf(f"window{i}", [P, T], F32) for i in range(2)]
+        w8_codes = sbuf("w8_codes", [P, M], U32)
+        w8_plane = sbuf("w8_plane", [P, M], U8)
+        w4_codes = sbuf("w4_codes", [P, 2 * M], U8)
+        w4_plane = sbuf("w4_plane", [P, M], U8)
+        bias = sbuf("bias", [P, ROW_TILES], F32)
+        bias_rows = sbuf("bias_rows", [P, P], F32)
+        identity = sbuf("identity", [P, P], F32)
+        picked1 = sbuf("picked1", [P, S], U32)
+        picked0_early = sbuf("picked0_early", [P, EARLY], U32)
+        picked_scales = sbuf("picked_scales", [P, S], U8)
+
+        def list_slice(offsets, j0, j1):
+            return offsets[:, j0 // STRIPE : j1 // STRIPE]
 
         nc.gpsimd.memset(scale_window[0:SCALE_BASE, :], 0)
-
-        w8_rows = w8.rearrange("(p j) n -> p j n", j=PACK)
-
-        def load_w8(h, tag):
-            raw = keep.tile([P, PACK, HALF], F32, name=f"w8_raw{h}", tag=tag, align_bytes=64)
-            nc.sync.dma_start(raw[:], w8_rows[:, :, h * HALF : (h + 1) * HALF])
-            return raw
-
         scale_rows = tab32[:, P * T : P * T + SCALE_ROWS * T // 4].rearrange("a (q w) -> q a w", q=SCALE_ROWS)
         nc.sync.dma_start(scale_window[SCALE_BASE:P, :], scale_rows)
         nc.sync.dma_start(gather_list[:], offs)
-        nc.sync.dma_start(words[0][:], table_words(0))
-        nc.sync.dma_start(words[1][:], table_words(1))
+        for a in (1, 0):
+            nc.sync.dma_start(words[a][:], tab32[a, 0 : P * T].rearrange("(p t) -> p t", p=P))
+
         nc.gpsimd.memset(bias_rows[:], 0.0)
         nc.sync.dma_start(bias_rows[0:ROW_TILES, :], b.rearrange("(m p) -> m p", p=P))
         w4_scale_rows = w4_scales.bitcast(I32)[0]
-        for quadrant in (0, 2, 1, 3):
+        for quadrant in QUADRANT_ORDER:
             nc.sync.dma_start(
                 w4_plane[:].bitcast(I32)[32 * quadrant : 32 * quadrant + 4, :],
                 w4_scale_rows[4 * quadrant : 4 * (quadrant + 1), :],
             )
-        w8_raw0 = load_w8(0, "late_picked")
+
+        w8_rows = w8.rearrange("(p j) n -> p j n", j=PACK)
+
+        def load_w8(n0, n1, tag):
+            raw = sbuf(f"w8_raw{n0}", [P, PACK, n1 - n0], F32, tag)
+            nc.sync.dma_start(raw[:], w8_rows[:, :, n0:n1])
+            return raw
+
+        def quantise_w8(n0, n1, raws, tag=None):
+            rounded = sbuf(f"w8_bf16_{n0}", [P, n1 - n0, PACK], BF16, tag)
+            width = (n1 - n0) // len(raws)
+            for part, raw in enumerate(raws):
+                nc.scalar.copy(
+                    rounded[:, part * width : (part + 1) * width, :].rearrange("p (c i) j -> p c j i", i=4),
+                    raw[:].rearrange("p j (c i) -> p c j i", i=4),
+                )
+            nc.vector.quantize_mx(
+                out=w8_codes[:, n0:n1].bitcast(FP8X4),
+                scales=w8_plane[:, n0:n1],
+                in_=rounded[:].rearrange("p n j -> p (n j)"),
+            )
+
+        w8_raw_first = [load_w8(0, P, None), load_w8(P, HALF, "late_picked")]
         nc.sync.dma_start(w4_codes[:].bitcast(I32), w4_words.bitcast(I32)[0])
-        nc.sync.dma_start(scatter_list[:], offs2)
         make_identity(nc, identity[:])
         for window in windows:
             nc.gpsimd.memset(window[:].bitcast(I32), 0)
@@ -93,93 +108,85 @@ def tile_list_tabscat_o_gelu_kernel(
         nc.tensor.transpose(bias_columns[:], bias_rows[:], identity[:])
         nc.scalar.copy(bias[:], bias_columns[:, 0:ROW_TILES])
 
-        def quantise_w8(h, raw, tag):
-            rounded = keep.tile([P, HALF, PACK], BF16, name=f"w8_bf16_{h}", tag=tag, align_bytes=64)
-            nc.scalar.copy(
-                rounded[:].rearrange("p (c i) j -> p c j i", i=4),
-                raw[:].rearrange("p j (c i) -> p c j i", i=4),
-            )
-            nc.vector.quantize_mx(
-                out=w8_codes[h][:].bitcast(FP8X4),
-                scales=w8_plane[h][:],
-                in_=rounded[:].rearrange("p n j -> p (n j)"),
-            )
-
-        def list_slice(offsets, j0, j1):
-            return offsets[:, j0 // STRIPE : j1 // STRIPE]
-
         nc.vector.tensor_copy(picked_scales[:], scale_window[:].bitcast(U8).indirect(gather_list[:]))
-        for quadrant in (0, 2, 1, 3):
-            nc.sync.dma_start(
-                planes[:].bitcast(I32)[32 * quadrant : 32 * quadrant + 4, :].rearrange("p (a w) -> p a w", a=2),
-                picked_scales[:].bitcast(I32)[SCALE_BASE + 8 * quadrant : SCALE_BASE + 8 * (quadrant + 1), :],
-            )
 
-        def plane(a, j0):
-            return planes[:, a * S + j0 : a * S + j0 + BANK]
+        def carry_planes(j0, j1):
+            planes = sbuf(f"planes{j0}", [P, 2 * (j1 - j0)], U8)
+            for quadrant in QUADRANT_ORDER:
+                nc.sync.dma_start(
+                    planes[:].bitcast(I32)[32 * quadrant : 32 * quadrant + 4, :].rearrange("p (a w) -> p a w", a=2),
+                    picked_scales[:].bitcast(I32)[
+                        SCALE_BASE + 8 * quadrant : SCALE_BASE + 8 * (quadrant + 1), j0 // 4 : j1 // 4
+                    ],
+                )
+            return planes
 
+        planes_first = carry_planes(0, BANK)
+        nc.sync.dma_start(scatter_list[:], offs2)
 
-        nc.vector.tensor_copy(picked0[:], words[0][:].bitcast(U32).indirect(gather_list[:]))
-        weight = keep.tile([P, S], F32, name="weight", tag="words0", align_bytes=64)
-        nc.sync.dma_start(weight[:, 0:FIRST], wgo[:, 0:FIRST])
-        nc.sync.dma_start(weight[:, FIRST:S], wgo[:, FIRST:S])
-        for j0 in range(0, EARLY, BANK):
-            nc.vector.tensor_copy(
-                picked1_early[:, j0 : j0 + BANK],
-                words[1][:].bitcast(U32).indirect(list_slice(gather_list, j0, j0 + BANK)),
-            )
-        quantise_w8(0, w8_raw0, "late_w8")
-        picked1_late = keep.tile([P, S - EARLY], U32, name="picked1_late", tag="late_picked", align_bytes=64)
+        nc.vector.tensor_copy(picked1[:], words[1][:].bitcast(U32).indirect(gather_list[:]))
+        weight = sbuf("weight", [P, S], F32, "words1")
+        nc.sync.dma_start(weight[:, 0:BANK], wgo[:, 0:BANK])
+        planes_rest = carry_planes(BANK, S)
         nc.vector.tensor_copy(
-            picked1_late[:], words[1][:].bitcast(U32).indirect(list_slice(gather_list, EARLY, S))
+            picked0_early[:], words[0][:].bitcast(U32).indirect(list_slice(gather_list, 0, EARLY))
         )
-        w8_raw1 = load_w8(1, "late_w8")
+        quantise_w8(0, HALF, w8_raw_first, "late_w8")
+        picked0_late = sbuf("picked0_late", [P, S - EARLY], U32, "late_picked")
+        nc.vector.tensor_copy(
+            picked0_late[:], words[0][:].bitcast(U32).indirect(list_slice(gather_list, EARLY, S))
+        )
+        nc.sync.dma_start(weight[:, BANK:S], wgo[:, BANK:S])
+        w8_raw_rest = [load_w8(HALF, HALF + P, "late_w8"), load_w8(HALF + P, M, "picked_scales")]
 
-        def fp4_pass(acc, m, j0):
-            if j0 < EARLY:
-                moving = picked1_early[:, j0 : j0 + BANK]
-            else:
-                moving = picked1_late[:, j0 - EARLY : j0 - EARLY + BANK]
-            nc.tensor.matmul_mx(
-                out=acc[:],
-                lhsT=w4_codes[:, 2 * m * P : 2 * (m + 1) * P].bitcast(FP4X4),
-                lhsT_scale=w4_plane[:, m * P : (m + 1) * P],
-                rhs=moving.bitcast(FP8X4),
-                rhs_scale=plane(1, j0),
-                start=True,
-                stop=False,
-            )
+        def plane(a, j):
+            if j < BANK:
+                return planes_first[:, a * BANK : (a + 1) * BANK]
+            c0 = a * (S - BANK) + j - BANK
+            return planes_rest[:, c0 : c0 + BANK]
 
-        def fp8_pass(acc, m, j0):
-            h, c0 = divmod(m * P, HALF)
-            nc.tensor.matmul_mx(
-                out=acc[:],
-                lhsT=w8_codes[h][:, c0 : c0 + P].bitcast(FP8X4),
-                lhsT_scale=w8_plane[h][:, c0 : c0 + P],
-                rhs=picked0[:, j0 : j0 + BANK].bitcast(FP8X4),
-                rhs_scale=plane(0, j0),
-                start=False,
-                stop=True,
-            )
+        def picked0(j):
+            if j < EARLY:
+                return picked0_early[:, j : j + BANK]
+            return picked0_late[:, j - EARLY : j - EARLY + BANK]
 
-        def piece(m, j0, j1):
-            values = keep.tile([P, j1 - j0], F32, name=f"values{m}_{j0}", tag=f"values{m}_{j0}", align_bytes=64)
+        def piece(m, j0, j1, tag=None):
+            rows = slice(m * P, (m + 1) * P)
+            values = sbuf(f"values{m}_{j0}", [P, j1 - j0], F32, tag)
             for j in range(j0, j1, BANK):
                 acc = psum.tile([P, BANK], F32, name="acc")
-                fp4_pass(acc, m, j)
-                fp8_pass(acc, m, j)
+                nc.tensor.matmul_mx(
+                    out=acc[:],
+                    lhsT=w4_codes[:, 2 * m * P : 2 * (m + 1) * P].bitcast(FP4X4),
+                    lhsT_scale=w4_plane[:, rows],
+                    rhs=picked1[:, j : j + BANK].bitcast(FP8X4),
+                    rhs_scale=plane(1, j),
+                    start=True,
+                    stop=False,
+                )
+                nc.tensor.matmul_mx(
+                    out=acc[:],
+                    lhsT=w8_codes[:, rows].bitcast(FP8X4),
+                    lhsT_scale=w8_plane[:, rows],
+                    rhs=picked0(j).bitcast(FP8X4),
+                    rhs_scale=plane(0, j),
+                    start=False,
+                    stop=True,
+                )
                 nc.scalar.activation(values[:, j - j0 : j - j0 + BANK], acc[:], GELU, bias=bias[:, m : m + 1])
             window = windows[m % 2]
             nc.vector.tensor_tensor(
                 window[:].indirect(list_slice(scatter_list, j0, j1)), values[:], weight[:, j0:j1], MULT
             )
             if j1 == S:
-                nc.sync.dma_start(out[m * P : (m + 1) * P, :], window[:])
+                parts = 1 if m == ROW_TILES - 1 else 2
+                for t0 in range(0, T, T // parts):
+                    nc.sync.dma_start(out[rows, t0 : t0 + T // parts], window[:, t0 : t0 + T // parts])
 
-        piece(0, 0, FIRST)
-        piece(1, 0, FIRST)
-        quantise_w8(1, w8_raw1, "values0_0")
-        piece(0, FIRST, S)
-        piece(1, FIRST, S)
+        piece(0, 0, BANK)
+        piece(1, 0, BANK)
+        quantise_w8(HALF, M, w8_raw_rest)
+        piece(0, BANK, S, "picked_scales")
+        piece(1, BANK, S)
         piece(2, 0, S)
         piece(3, 0, S)

@@ -90,7 +90,7 @@ def tile_list_tabscat_o_gelu_kernel(
             for part, raw in enumerate(raws):
                 nc.scalar.copy(
                     rounded[:, part * width : (part + 1) * width, :].rearrange("p (c i) j -> p c j i", i=4),
-                    raw[:].rearrange("p j (c i) -> p c j i", i=4),
+                    raw.rearrange("p j (c i) -> p c j i", i=4),
                 )
             nc.vector.quantize_mx(
                 out=w8_codes[:, n0:n1].bitcast(FP8X4),
@@ -98,9 +98,11 @@ def tile_list_tabscat_o_gelu_kernel(
                 in_=rounded[:].rearrange("p n j -> p (n j)"),
             )
 
-        w8_raw_first = [load_w8(0, P, None), load_w8(P, HALF, "late_picked")]
+        w8_raw_first = load_w8(0, HALF, "late_picked")
         nc.sync.dma_start(w4_codes[:].bitcast(I32), w4_words.bitcast(I32)[0])
         make_identity(nc, identity[:])
+        warm = sbuf("warm", [P, 1], F32)
+        nc.scalar.activation(warm[:], identity[:, 0:1], GELU)
         for window in windows:
             nc.gpsimd.memset(window[:].bitcast(I32), 0)
 
@@ -131,13 +133,14 @@ def tile_list_tabscat_o_gelu_kernel(
         nc.vector.tensor_copy(
             picked0_early[:], words[0][:].bitcast(U32).indirect(list_slice(gather_list, 0, EARLY))
         )
-        quantise_w8(0, HALF, w8_raw_first, "late_w8")
+        quantise_w8(0, P, [w8_raw_first[:, :, 0:P]], "late_w8")
         picked0_late = sbuf("picked0_late", [P, S - EARLY], U32, "late_picked")
         nc.vector.tensor_copy(
             picked0_late[:], words[0][:].bitcast(U32).indirect(list_slice(gather_list, EARLY, S))
         )
+        quantise_w8(P, HALF, [w8_raw_first[:, :, P:HALF]])
         nc.sync.dma_start(weight[:, BANK:S], wgo[:, BANK:S])
-        w8_raw_rest = [load_w8(HALF, HALF + P, "late_w8"), load_w8(HALF + P, M, "picked_scales")]
+        w8_raw_rest = [load_w8(HALF, HALF + P, "late_w8")[:], load_w8(HALF + P, M, "picked_scales")[:]]
 
         def plane(a, j):
             if j < BANK:

@@ -101,8 +101,6 @@ def tile_list_tabscat_o_gelu_kernel(
         w8_raw_first = load_w8(0, HALF, "late_picked")
         nc.sync.dma_start(w4_codes[:].bitcast(I32), w4_words.bitcast(I32)[0])
         make_identity(nc, identity[:])
-        warm = sbuf("warm", [P, 1], F32)
-        nc.scalar.activation(warm[:], identity[:, 0:1], GELU)
         for window in windows:
             nc.gpsimd.memset(window[:].bitcast(I32), 0)
 

@@ -98,7 +98,7 @@ def tile_list_tabscat_o_gelu_kernel(
                 in_=rounded[:].rearrange("p n j -> p (n j)"),
             )
 
-        w8_raw_first = load_w8(0, HALF, "late_picked")
+        w8_raw_first = [load_w8(0, P, "late_picked"), load_w8(P, HALF, None)]
         nc.sync.dma_start(w4_codes[:].bitcast(I32), w4_words.bitcast(I32)[0])
         make_identity(nc, identity[:])
         for window in windows:
@@ -131,12 +131,12 @@ def tile_list_tabscat_o_gelu_kernel(
         nc.vector.tensor_copy(
             picked0_early[:], words[0][:].bitcast(U32).indirect(list_slice(gather_list, 0, EARLY))
         )
-        quantise_w8(0, P, [w8_raw_first[:, :, 0:P]], "late_w8")
+        quantise_w8(0, P, [w8_raw_first[0][:]], "late_w8")
         picked0_late = sbuf("picked0_late", [P, S - EARLY], U32, "late_picked")
         nc.vector.tensor_copy(
             picked0_late[:], words[0][:].bitcast(U32).indirect(list_slice(gather_list, EARLY, S))
         )
-        quantise_w8(P, HALF, [w8_raw_first[:, :, P:HALF]])
+        quantise_w8(P, HALF, [w8_raw_first[1][:]])
         nc.sync.dma_start(weight[:, BANK:S], wgo[:, BANK:S])
         w8_raw_rest = [load_w8(HALF, HALF + P, "late_w8")[:], load_w8(HALF + P, M, "picked_scales")[:]]
 

@@ -16,6 +16,7 @@ FP8X4 = mybir.dt.float8_e4m3fn_x4
 FP4X4 = mybir.dt.float4_e2m1fn_x4
 GELU = mybir.ActivationFunctionType.Gelu_apprx_tanh
 MULT = mybir.AluOpType.mult
+ADD = mybir.AluOpType.add
 
 P = 128
 PACK = 4
@@ -84,21 +85,23 @@ def tile_list_tabscat_o_gelu_kernel(
             nc.sync.dma_start(raw[:], w8_rows[:, :, n0:n1])
             return raw
 
-        def quantise_w8(n0, n1, raws, tag=None):
+        def quantise_w8(n0, n1, raws, tag=None, on_gpsimd=False):
             rounded = sbuf(f"w8_bf16_{n0}", [P, n1 - n0, PACK], BF16, tag)
             width = (n1 - n0) // len(raws)
             for part, raw in enumerate(raws):
-                nc.scalar.copy(
-                    rounded[:, part * width : (part + 1) * width, :].rearrange("p (c i) j -> p c j i", i=4),
-                    raw.rearrange("p j (c i) -> p c j i", i=4),
-                )
+                dst = rounded[:, part * width : (part + 1) * width, :].rearrange("p (c i) j -> p c j i", i=4)
+                src = raw.rearrange("p j (c i) -> p c j i", i=4)
+                if on_gpsimd:
+                    nc.gpsimd.tensor_scalar(dst, src, 1.0, 0.0, MULT, ADD)
+                else:
+                    nc.scalar.copy(dst, src)
             nc.vector.quantize_mx(
                 out=w8_codes[:, n0:n1].bitcast(FP8X4),
                 scales=w8_plane[:, n0:n1],
                 in_=rounded[:].rearrange("p n j -> p (n j)"),
             )
 
-        w8_raw_first = [load_w8(0, P, "late_picked"), load_w8(P, HALF, None)]
+        w8_raw_tile0 = load_w8(0, P, "late_picked")
         nc.sync.dma_start(w4_codes[:].bitcast(I32), w4_words.bitcast(I32)[0])
         make_identity(nc, identity[:])
         for window in windows:
@@ -122,6 +125,7 @@ def tile_list_tabscat_o_gelu_kernel(
             return planes
 
         planes_first = carry_planes(0, BANK)
+        w8_raw_tile1 = load_w8(P, HALF, "scale_window")
         nc.sync.dma_start(scatter_list[:], offs2)
 
         nc.vector.tensor_copy(picked1[:], words[1][:].bitcast(U32).indirect(gather_list[:]))
@@ -131,14 +135,14 @@ def tile_list_tabscat_o_gelu_kernel(
         nc.vector.tensor_copy(
             picked0_early[:], words[0][:].bitcast(U32).indirect(list_slice(gather_list, 0, EARLY))
         )
-        quantise_w8(0, P, [w8_raw_first[0][:]], "late_w8")
+        quantise_w8(0, P, [w8_raw_tile0[:]], "late_w8")
         picked0_late = sbuf("picked0_late", [P, S - EARLY], U32, "late_picked")
         nc.vector.tensor_copy(
             picked0_late[:], words[0][:].bitcast(U32).indirect(list_slice(gather_list, EARLY, S))
         )
-        quantise_w8(P, HALF, [w8_raw_first[1][:]])
+        quantise_w8(P, HALF, [w8_raw_tile1[:]], on_gpsimd=True)
         nc.sync.dma_start(weight[:, BANK:S], wgo[:, BANK:S])
-        w8_raw_rest = [load_w8(HALF, HALF + P, "late_w8")[:], load_w8(HALF + P, M, "picked_scales")[:]]
+        w8_raw_rest = [load_w8(HALF, M, "late_w8")[:]]
 
         def plane(a, j):
             if j < BANK:
@@ -187,7 +191,7 @@ def tile_list_tabscat_o_gelu_kernel(
         piece(0, 0, BANK)
         piece(1, 0, BANK)
         quantise_w8(HALF, M, w8_raw_rest)
-        piece(0, BANK, S, "picked_scales")
+        piece(0, BANK, S, "late_w8")
         piece(1, BANK, S)
         piece(2, 0, S)
         piece(3, 0, S)

from contextlib import ExitStack

import concourse.mybir as mybir
from concourse.masks import make_identity

K, M, T, S = 1024, 512, 4096, 2048
FLOPS = 2 * K * M * S

F32 = mybir.dt.float32
BF16 = mybir.dt.bfloat16
I32 = mybir.dt.int32
U32 = mybir.dt.uint32
U16 = mybir.dt.uint16
U8 = mybir.dt.uint8
FP8X4 = mybir.dt.float8_e4m3fn_x4
FP4X4 = mybir.dt.float4_e2m1fn_x4
GELU = mybir.ActivationFunctionType.Gelu_apprx_tanh
MULT = mybir.AluOpType.mult
ADD = mybir.AluOpType.add

P = 128
PACK = 4
BANK = 512
STRIPE = 16
ROW_TILES = M // P
HALF = M // 2
EARLY = 1024
SCALE_ROWS = 16
SCALE_BASE = P - 2 * SCALE_ROWS
QUADRANT_ORDER = (0, 2, 1, 3)


def tile_list_tabscat_o_gelu_kernel(
    tc, tab, w8, w4_words, w4_scales, b, wgo, offs, offs2, out
):
    nc = tc.nc
    with ExitStack() as ctx:
        keep = ctx.enter_context(tc.tile_pool(name="keep", bufs=1))
        psum = ctx.enter_context(tc.psum_pool(name="psum", bufs=2))
        psum_bias = ctx.enter_context(tc.psum_pool(name="psum_bias", bufs=1))

        def sbuf(name, shape, dtype, tag=None):
            return keep.tile(shape, dtype, name=name, tag=tag or name, align_bytes=64)

        tab32 = tab.bitcast(I32)
        gather_list = keep.tile([P, S // STRIPE], U16, name="gather_list")
        scatter_list = keep.tile([P, S // STRIPE], U16, name="scatter_list")
        words = [sbuf(f"words{a}", [P, T], I32) for a in range(2)]
        scale_window = sbuf("scale_window", [P, T // 4], I32)
        windows = [sbuf(f"window{i}", [P, T], F32) for i in range(2)]
        w8_codes = sbuf("w8_codes", [P, M], U32)
        w8_plane = sbuf("w8_plane", [P, M], U8)
        w4_codes = sbuf("w4_codes", [P, 2 * M], U8)
        w4_plane = sbuf("w4_plane", [P, M], U8)
        bias = sbuf("bias", [P, ROW_TILES], F32)
        bias_rows = sbuf("bias_rows", [P, P], F32)
        identity = sbuf("identity", [P, P], F32)
        picked1 = sbuf("picked1", [P, S], U32)
        picked0_early = sbuf("picked0_early", [P, EARLY], U32)
        picked_scales = sbuf("picked_scales", [P, S], U8)

        def list_slice(offsets, j0, j1):
            return offsets[:, j0 // STRIPE : j1 // STRIPE]

        nc.gpsimd.memset(scale_window[0:SCALE_BASE, :], 0)
        scale_rows = tab32[:, P * T : P * T + SCALE_ROWS * T // 4].rearrange("a (q w) -> q a w", q=SCALE_ROWS)
        nc.sync.dma_start(scale_window[SCALE_BASE:P, :], scale_rows)
        nc.sync.dma_start(gather_list[:], offs)
        for a in (1, 0):
            nc.sync.dma_start(words[a][:], tab32[a, 0 : P * T].rearrange("(p t) -> p t", p=P))

        nc.gpsimd.memset(bias_rows[:], 0.0)
        nc.sync.dma_start(bias_rows[0:ROW_TILES, :], b.rearrange("(m p) -> m p", p=P))
        w4_scale_rows = w4_scales.bitcast(I32)[0]
        for quadrant in QUADRANT_ORDER:
            nc.sync.dma_start(
                w4_plane[:].bitcast(I32)[32 * quadrant : 32 * quadrant + 4, :],
                w4_scale_rows[4 * quadrant : 4 * (quadrant + 1), :],
            )

        w8_rows = w8.rearrange("(p j) n -> p j n", j=PACK)

        def load_w8(n0, n1, tag):
            raw = sbuf(f"w8_raw{n0}", [P, PACK, n1 - n0], F32, tag)
            nc.sync.dma_start(raw[:], w8_rows[:, :, n0:n1])
            return raw

        def quantise_w8(n0, n1, raws, tag=None, on_gpsimd=False):
            rounded = sbuf(f"w8_bf16_{n0}", [P, n1 - n0, PACK], BF16, tag)
            width = (n1 - n0) // len(raws)
            for part, raw in enumerate(raws):
                dst = rounded[:, part * width : (part + 1) * width, :].rearrange("p (c i) j -> p c j i", i=4)
                src = raw.rearrange("p j (c i) -> p c j i", i=4)
                if on_gpsimd:
                    nc.gpsimd.tensor_scalar(dst, src, 1.0, 0.0, MULT, ADD)
                else:
                    nc.scalar.copy(dst, src)
            nc.vector.quantize_mx(
                out=w8_codes[:, n0:n1].bitcast(FP8X4),
                scales=w8_plane[:, n0:n1],
                in_=rounded[:].rearrange("p n j -> p (n j)"),
            )

        w8_raw_tile0 = load_w8(0, P, "late_picked")
        nc.sync.dma_start(w4_codes[:].bitcast(I32), w4_words.bitcast(I32)[0])
        make_identity(nc, identity[:])
        for window in windows:
            nc.gpsimd.memset(window[:].bitcast(I32), 0)

        bias_columns = psum_bias.tile([P, P], F32, name="bias_columns")
        nc.tensor.transpose(bias_columns[:], bias_rows[:], identity[:])
        nc.scalar.copy(bias[:], bias_columns[:, 0:ROW_TILES])

        nc.vector.tensor_copy(picked_scales[:], scale_window[:].bitcast(U8).indirect(gather_list[:]))

        def carry_planes(j0, j1):
            planes = sbuf(f"planes{j0}", [P, 2 * (j1 - j0)], U8)
            for quadrant in QUADRANT_ORDER:
                nc.sync.dma_start(
                    planes[:].bitcast(I32)[32 * quadrant : 32 * quadrant + 4, :].rearrange("p (a w) -> p a w", a=2),
                    picked_scales[:].bitcast(I32)[
                        SCALE_BASE + 8 * quadrant : SCALE_BASE + 8 * (quadrant + 1), j0 // 4 : j1 // 4
                    ],
                )
            return planes

        planes_first = carry_planes(0, BANK)
        w8_raw_tile1 = load_w8(P, HALF, "scale_window")
        nc.sync.dma_start(scatter_list[:], offs2)

        nc.vector.tensor_copy(picked1[:], words[1][:].bitcast(U32).indirect(gather_list[:]))
        weight = sbuf("weight", [P, S], F32, "words1")
        nc.sync.dma_start(weight[:, 0:BANK], wgo[:, 0:BANK])
        planes_rest = carry_planes(BANK, S)
        nc.vector.tensor_copy(
            picked0_early[:], words[0][:].bitcast(U32).indirect(list_slice(gather_list, 0, EARLY))
        )
        quantise_w8(0, P, [w8_raw_tile0[:]], "late_w8")
        picked0_late = sbuf("picked0_late", [P, S - EARLY], U32, "late_picked")
        nc.vector.tensor_copy(
            picked0_late[:], words[0][:].bitcast(U32).indirect(list_slice(gather_list, EARLY, S))
        )
        quantise_w8(P, HALF, [w8_raw_tile1[:]], on_gpsimd=True)
        nc.sync.dma_start(weight[:, BANK:S], wgo[:, BANK:S])
        w8_raw_rest = [load_w8(HALF, M, "late_w8")[:]]

        def plane(a, j):
            if j < BANK:
                return planes_first[:, a * BANK : (a + 1) * BANK]
            c0 = a * (S - BANK) + j - BANK
            return planes_rest[:, c0 : c0 + BANK]

        def picked0(j):
            if j < EARLY:
                return picked0_early[:, j : j + BANK]
            return picked0_late[:, j - EARLY : j - EARLY + BANK]

        def piece(m, j0, j1, tag=None):
            rows = slice(m * P, (m + 1) * P)
            values = sbuf(f"values{m}_{j0}", [P, j1 - j0], F32, tag)
            for j in range(j0, j1, BANK):
                acc = psum.tile([P, BANK], F32, name="acc")
                nc.tensor.matmul_mx(
                    out=acc[:],
                    lhsT=w4_codes[:, 2 * m * P : 2 * (m + 1) * P].bitcast(FP4X4),
                    lhsT_scale=w4_plane[:, rows],
                    rhs=picked1[:, j : j + BANK].bitcast(FP8X4),
                    rhs_scale=plane(1, j),
                    start=True,
                    stop=False,
                )
                nc.tensor.matmul_mx(
                    out=acc[:],
                    lhsT=w8_codes[:, rows].bitcast(FP8X4),
                    lhsT_scale=w8_plane[:, rows],
                    rhs=picked0(j).bitcast(FP8X4),
                    rhs_scale=plane(0, j),
                    start=False,
                    stop=True,
                )
                nc.scalar.activation(values[:, j - j0 : j - j0 + BANK], acc[:], GELU, bias=bias[:, m : m + 1])
            window = windows[m % 2]
            nc.vector.tensor_tensor(
                window[:].indirect(list_slice(scatter_list, j0, j1)), values[:], weight[:, j0:j1], MULT
            )
            if j1 == S:
                parts = 1 if m == ROW_TILES - 1 else 2
                for t0 in range(0, T, T // parts):
                    nc.sync.dma_start(out[rows, t0 : t0 + T // parts], window[:, t0 : t0 + T // parts])

        piece(0, 0, BANK)
        piece(1, 0, BANK)
        quantise_w8(HALF, M, w8_raw_rest)
        piece(0, BANK, S, "late_w8")
        piece(1, BANK, S)
        piece(2, 0, S)
        piece(3, 0, S)
